import numpy as np
import ml_dtypes


def mxq(x, axis, fmt="e4m3"):
    dtype, down = {"e4m3": (ml_dtypes.float8_e4m3fn, 7), "e5m2": (ml_dtypes.float8_e5m2, 14)}[fmt]
    v = np.moveaxis(np.asarray(x, np.float32).astype(ml_dtypes.bfloat16).astype(np.float64), axis, -1)
    blocks = v.reshape(v.shape[:-1] + (-1, 32))
    amax = np.abs(blocks).max(-1, keepdims=True)
    byte = np.maximum(np.where(amax > 0, np.frexp(amax)[1] - 1 + 127, 0) - down, 1)
    scale = np.exp2(byte - 127.0)
    codes = (blocks / scale).astype(np.float32).astype(dtype).astype(np.float64)
    return np.moveaxis((codes * scale).reshape(v.shape), -1, axis)


WIDE = False


def mx_kscale(k):
    if not WIDE:
        return np.ones(k)
    levels = np.array([30, -30])
    if k % 512:
        return np.exp2(np.random.permutation(np.resize(levels, k // 32))).repeat(32)
    a = np.empty((k // 512, 16))
    for p in range(k // 512):
        a[p, :8] = np.random.permutation(np.resize(levels, 8))
        for g in range(8):
            far = levels[np.abs(levels - a[p, g]) >= 10]
            a[p, g + 8] = far[np.random.randint(len(far))]
    return np.exp2(a.ravel()).repeat(32)


def f64(x):
    return np.asarray(x).astype(np.float64)


def striped(idx):
    return np.tile(np.asarray(idx).reshape(-1, 16).T, (8, 1)).astype(np.uint16)


def unstriped(offs):
    return offs[:16].T.reshape(-1).astype(np.int64)


E2M1 = np.array([0.0, 0.5, 1.0, 1.5, 2.0, 3.0, 4.0, 6.0, -0.0, -0.5, -1.0, -1.5, -2.0, -3.0, -4.0, -6.0])


def pack_weight(w, fmt):
    k, n = w.shape
    w = f64(np.asarray(w, np.float32).astype(ml_dtypes.bfloat16)).reshape(k // 32, 32, n)
    amax = np.abs(w).max(1)
    if fmt in ("e4m3", "e5m2"):
        byte = np.frexp(amax)[1] - 1 + 127 - (7 if fmt == "e4m3" else 14)
    else:
        mant, ex = np.frexp(amax / 6.0)
        byte = np.where(mant > 0.5, ex, ex - 1) + 127
    byte = np.clip(np.where(amax > 0, byte, 1), 1, 254)
    scaled = (w * np.exp2(127.0 - byte)[:, None, :]).reshape(k, n).astype(np.float32)
    by_word = np.ascontiguousarray(scaled.reshape(k // 512, 128, 4, n).transpose(0, 1, 3, 2))
    if fmt in ("e4m3", "e5m2"):
        words = by_word.astype(ml_dtypes.float8_e4m3fn if fmt == "e4m3" else ml_dtypes.float8_e5m2).view(np.uint8)
    else:
        c = by_word.astype(ml_dtypes.float4_e2m1fn).view(np.uint8) & 0xF
        words = (c[..., 0::2] | (c[..., 1::2] << 4)).reshape(k // 512, 128, 2 * n)
    return np.ascontiguousarray(words), np.ascontiguousarray(byte.astype(np.uint8).reshape(k // 512, 16, n))


def unpack_weight(words, scales, fmt):
    g, _, n = scales.shape
    words = np.ascontiguousarray(words).reshape(g, 128, n, -1)
    if fmt in ("e4m3", "e5m2"):
        vals = words.view(ml_dtypes.float8_e4m3fn if fmt == "e4m3" else ml_dtypes.float8_e5m2).astype(np.float64)
    else:
        nib = np.empty((g, 128, n, 4), np.uint8)
        nib[..., 0::2] = words & 0xF
        nib[..., 1::2] = words >> 4
        vals = E2M1[nib]
    vals = vals * np.repeat(np.exp2(scales.astype(np.float64) - 127.0), 8, axis=1)[..., None]
    return vals.transpose(0, 1, 3, 2).reshape(g * 512, n)


K, T, J, R, C, I, O, N = 512, 1024, 256, 512, 512, 128, 128, 256


def setup_inputs():
    n = np.random.standard_normal
    idx = np.random.permutation(T)[:J]
    idx2 = np.random.permutation(C)[:J]
    idx3 = np.random.permutation(J)[:I]
    idx4 = np.random.permutation(C)[:I]
    idx5 = np.random.permutation(C)[:O]
    idx6 = np.random.permutation(C)[:O]
    idx7 = np.random.permutation(T)[:O]
    fk = mx_kscale(K)
    fr = mx_kscale(R)
    xtp = pack_weight(n((K, T)) / fk[:, None], "e5m2")
    wp = pack_weight(n((K, R)) * 1 / np.sqrt(K) * fk[:, None] * fr, "e2m1")
    w2p = pack_weight(n((K, R)) * 1 / np.sqrt(K) * fk[:, None], "e4m3")
    wbp = pack_weight(n((R, N)) * 1 / np.sqrt(R) / fr[:, None], "e2m1")
    wsp = pack_weight(n((K, N)) * 1 / np.sqrt(K) * fk[:, None], "e2m1")
    return {
        "xt_words": xtp[0],
        "xt_scales": xtp[1],
        "w_words": wp[0],
        "w_scales": wp[1],
        "w2_words": w2p[0],
        "w2_scales": w2p[1],
        "wb_words": wbp[0],
        "wb_scales": wbp[1],
        "ws_words": wsp[0],
        "ws_scales": wsp[1],
        "offs": striped(idx),
        "offs2": striped(idx2),
        "offs3": striped(idx3),
        "offs4": striped(idx4),
        "offs5": striped(idx5),
        "offs6": striped(idx6),
        "offs7": striped(idx7),
    }


def reference(xt_words, xt_scales, w_words, w_scales, w2_words, w2_scales, wb_words, wb_scales, ws_words, ws_scales, offs, offs2, offs3, offs4, offs5, offs6, offs7):
    idx = unstriped(offs)
    idx2 = unstriped(offs2)
    idx3 = unstriped(offs3)
    idx4 = unstriped(offs4)
    idx5 = unstriped(offs5)
    idx6 = unstriped(offs6)
    idx7 = unstriped(offs7)
    xtu = unpack_weight(xt_words, xt_scales, "e5m2")
    wu = unpack_weight(w_words, w_scales, "e2m1")
    w2u = unpack_weight(w2_words, w2_scales, "e4m3")
    wbu = unpack_weight(wb_words, wb_scales, "e2m1")
    wsu = unpack_weight(ws_words, ws_scales, "e2m1")
    xtidxg = xtu[:, idx]
    a = wu.T @ xtidxg
    b = w2u.T @ xtidxg
    lb = b[:, 0:1]
    la = a[:, 0:1]
    pw = np.zeros((R, C))
    pw[:, idx2] = a
    h1 = b[:, idx3] * la
    pv = np.zeros((R, C))
    pv[:, idx4] = h1
    pg = pw + pv
    hid = np.abs(pg[:, idx5] * lb - pg[:, idx6])
    hidq = mxq(hid, 0, "e4m3")
    xtidx7g = xtu[:, idx7]
    y = wbu.T @ hidq + wsu.T @ xtidx7g
    return y

@@ -1,0 +1,236 @@
+from contextlib import ExitStack
+
+import concourse.mybir as mybir
+
+K, T, J, R, C, I, O, N = 512, 1024, 256, 512, 512, 128, 128, 256
+FLOPS = 2 * K * R * J * 2 + 2 * R * N * O + 2 * K * N * O
+
+F32 = mybir.dt.float32
+BF16 = mybir.dt.bfloat16
+I32 = mybir.dt.int32
+U32 = mybir.dt.uint32
+U16 = mybir.dt.uint16
+U8 = mybir.dt.uint8
+E4M3 = mybir.dt.float8_e4m3fn_x4
+E5M2 = mybir.dt.float8_e5m2_x4
+E2M1 = mybir.dt.float4_e2m1fn_x4
+ACT = mybir.ActivationFunctionType
+ALU = mybir.AluOpType
+
+P = 128
+PACK = 4
+QUAD = 32
+
+
+def tile_list_leadshared_twow_further_plain_kernel(
+    tc, xt_words, xt_scales, w_words, w_scales, w2_words, w2_scales, wb_words, wb_scales,
+    ws_words, ws_scales, offs, offs2, offs3, offs4, offs5, offs6, offs7, out,
+):
+    nc = tc.nc
+    with ExitStack() as ctx:
+        keep = ctx.enter_context(tc.tile_pool(name="keep", bufs=1))
+        psum = ctx.enter_context(tc.psum_pool(name="psum", bufs=1))
+
+        def sb(name, shape, dtype, tag=None):
+            return keep.tile(shape, dtype, name=name, tag=tag or name, align_bytes=64)
+
+        def load_list(name, src):
+            lst = sb(name, list(src.shape), U16)
+            nc.sync.dma_start(lst[:], src)
+            return lst
+
+        def zero_plane(name, width):
+            plane = sb(name, [P, width // 4], I32)
+            nc.vector.memset(plane[:], 0)
+            return plane
+
+        def load_plane(queue, plane, scales):
+            rows = scales[0].bitcast(I32).rearrange("(q r) n -> r q n", r=PACK)
+            for r in range(PACK):
+                queue.dma_start(plane[r:P:QUAD, :], rows[r])
+
+        def load_full_plane(queue, name, scales):
+            rows = scales[0].bitcast(I32)
+            plane = sb(name, [P, rows.shape[1]], I32)
+            for q in range(PACK):
+                queue.dma_start(
+                    plane[QUAD * q : QUAD * (q + 1), :],
+                    rows[PACK * q : PACK * (q + 1), :].partition_broadcast(QUAD // PACK),
+                )
+            return plane
+
+        def zero_board(eng, name, tag=None):
+            board = sb(name, [P, C], F32, tag)
+            eng.memset(board[:], 0.0)
+            return board
+
+        w_plane = zero_plane("w_plane", R)
+        l_slot = load_list("l_slot", offs)
+        w_stage = sb("w_stage", [PACK, PACK, R // 4], I32)
+        nc.scalar.dma_start(w_stage[:], w_scales[0].bitcast(I32).rearrange("(q r) n -> r q n", r=PACK))
+        x_plane = load_full_plane(nc.sync, "x_plane", xt_scales)
+        x_words = sb("x_words", [P, T], I32)
+        nc.scalar.dma_start(x_words[:], xt_words[0].rearrange("p n t -> p (n t)").bitcast(I32))
+        w_raw = sb("w_raw", [P, R // 2], I32)
+        nc.scalar.dma_start(w_raw[:], w_words[0].bitcast(I32))
+        l_put_a = load_list("l_put_a", offs2)
+        l_short = load_list("l_short", offs7)
+        w2_raw = sb("w2_raw", [P, R], I32)
+        nc.sync.dma_start(w2_raw[:], w2_words[0].rearrange("p n t -> p (n t)").bitcast(I32))
+        w2_plane = load_full_plane(nc.sync, "w2_plane", w2_scales)
+        l_seat = load_list("l_seat", offs3)
+        l_put_h = load_list("l_put_h", offs4)
+        ws_plane = sb("ws_plane", [P, N // 4], I32)
+        wb_plane = sb("wb_plane", [P, N // 4], I32)
+        ws_raw = sb("ws_raw", [P, N // 2], I32)
+        nc.sync.dma_start(ws_raw[:], ws_words[0].bitcast(I32))
+        load_plane(nc.sync, ws_plane, ws_scales)
+        l_scaled = load_list("l_scaled", offs5)
+        l_plain = load_list("l_plain", offs6)
+        wb_raw = sb("wb_raw", [P, N // 2], I32)
+        nc.sync.dma_start(wb_raw[:], wb_words[0].bitcast(I32))
+        load_plane(nc.sync, wb_plane, wb_scales)
+
+        pw = [zero_board(nc.vector, "pw%d" % t) for t in range(PACK)]
+
+        for q in range(PACK):
+            nc.vector.tensor_copy(w_plane[QUAD * q : QUAD * q + PACK, :], w_stage[:, q, :])
+        xg_scale = sb("xg_scale", [P, J], U8)
+        nc.vector.tensor_copy(xg_scale[:], x_plane[:].bitcast(U8).indirect(l_slot[:]))
+        w_codes = [sb("w_codes%d" % t, [P, 2 * P], U8) for t in range(PACK)]
+        w_scale = [sb("w_scale%d" % t, [P, P], U8) for t in range(PACK)]
+        for t in range(PACK):
+            nc.scalar.copy(w_codes[t][:].bitcast(U16), w_raw[:].bitcast(U16)[:, t:R:PACK])
+        nc.vector.tensor_copy(w_scale[0][:], w_plane[:].bitcast(U8)[:, 0:R:PACK])
+        xg_words = sb("xg_words", [P, J], U32)
+        nc.vector.tensor_copy(xg_words[:], x_words[:].bitcast(U32).indirect(l_slot[:]))
+        for t in range(1, PACK):
+            nc.vector.tensor_copy(w_scale[t][:], w_plane[:].bitcast(U8)[:, t:R:PACK])
+        w2_codes = sb("w2_codes", [P, R], U32)
+        nc.scalar.copy(
+            w2_codes[:].rearrange("p (t c i) -> p c t i", t=PACK, i=4),
+            w2_raw[:].bitcast(U32).rearrange("p (c i t) -> p c t i", t=PACK, i=4),
+        )
+        w2_scale = [sb("w2_scale%d" % t, [P, P], U8) for t in range(PACK)]
+        for t in range(PACK):
+            nc.gpsimd.tensor_copy(w2_scale[t][:], w2_plane[:].bitcast(U8)[:, t:R:PACK])
+
+        a_ps = []
+        for t in range(PACK):
+            acc = psum.tile([P, J], F32, name="a_ps%d" % t, tag="bank%d" % t)
+            nc.tensor.matmul_mx(
+                out=acc[:], lhsT=w_codes[t][:].bitcast(E2M1), lhsT_scale=w_scale[t][:],
+                rhs=xg_words[:].bitcast(E5M2), rhs_scale=xg_scale[:], start=True, stop=True,
+            )
+            a_ps.append(acc)
+
+        a_sb = {}
+        b_sb = [sb("b_sb%d" % t, [P, J], F32) for t in range(PACK)]
+        h_sb = {}
+        pv = [zero_board(nc.gpsimd, "pv%d" % t, "w_codes%d" % t) for t in range(PACK)]
+        pg = [sb("pg%d" % t, [P, C], F32) for t in range(PACK)]
+        g5 = [sb("g5_%d" % t, [P, O], F32) for t in range(PACK)]
+        diff = sb("diff", [P, PACK, O], F32)
+
+        def copy_on(on_vector, dst, src):
+            if on_vector:
+                nc.vector.tensor_copy(dst, src)
+            else:
+                nc.scalar.activation(out=dst, in_=src, func=ACT.Copy)
+
+        def second_product(t):
+            acc = psum.tile([P, J], F32, name="b_ps%d" % t, tag="bank%d" % ((t + 4) % 6))
+            cols = slice(P * t, P * (t + 1))
+            nc.tensor.matmul_mx(
+                out=acc[:], lhsT=w2_codes[:, cols].bitcast(E4M3), lhsT_scale=w2_scale[t][:],
+                rhs=xg_words[:].bitcast(E5M2), rhs_scale=xg_scale[:], start=True, stop=True,
+            )
+            nc.vector.tensor_copy(b_sb[t][:], acc[:])
+
+        def fetch_a(t):
+            a_sb[t] = sb("a_sb%d" % t, [P, J], F32, "h_sb%d" % (t - 2) if t >= 2 else None)
+            copy_on(t % 2 == 0, a_sb[t][:], a_ps[t][:])
+
+        def put_a(t):
+            copy_on(t % 2 == 0, pw[t][:].indirect(l_put_a[:]), a_sb[t][:])
+
+        def seats(t):
+            h_sb[t] = sb("h_sb%d" % t, [P, I], F32, "b_sb1" if t == PACK - 1 else None)
+            nc.scalar.activation(
+                out=h_sb[t][:], in_=b_sb[t][:].indirect(l_seat[:]), func=ACT.Copy, scale=a_sb[t][:, 0:1]
+            )
+
+        def put_h(t):
+            copy_on(t % 2 == 0, pv[t][:].indirect(l_put_h[:]), h_sb[t][:])
+
+        def board(t):
+            eng = nc.vector if t == PACK - 1 else nc.gpsimd
+            eng.tensor_tensor(pg[t][:], pw[t][:], pv[t][:], ALU.add)
+
+        def places(t):
+            nc.scalar.activation(
+                out=g5[t][:], in_=pg[t][:].indirect(l_scaled[:]), func=ACT.Copy, scale=b_sb[t][:, 0:1]
+            )
+            nc.vector.tensor_tensor(diff[:, t, :], pg[t][:].indirect(l_plain[:]), g5[t][:], ALU.subtract)
+
+        fetch_a(0)
+        fetch_a(1)
+        put_a(0)
+        put_a(1)
+        for t in range(PACK):
+            second_product(t)
+
+        xs_scale = sb("xs_scale", [P, O], U8, "w_scale0")
+        nc.vector.tensor_copy(xs_scale[:], x_plane[:].bitcast(U8).indirect(l_short[:]))
+        xs_words = sb("xs_words", [P, O], U32)
+        nc.vector.tensor_copy(xs_words[:], x_words[:].bitcast(U32).indirect(l_short[:]))
+        y_ps = []
+        for h in range(N // P):
+            acc = psum.tile([P, O], F32, name="y_ps%d" % h, tag="out_bank%d" % h)
+            nc.tensor.matmul_mx(
+                out=acc[:], lhsT=ws_raw[:].bitcast(U8)[:, 2 * P * h : 2 * P * (h + 1)].bitcast(E2M1),
+                lhsT_scale=ws_plane[:].bitcast(U8)[:, P * h : P * (h + 1)],
+                rhs=xs_words[:].bitcast(E5M2), rhs_scale=xs_scale[:], start=True, stop=False,
+            )
+            y_ps.append(acc)
+
+        seats(0)
+        seats(1)
+        put_h(0)
+        put_h(1)
+        board(0)
+        board(1)
+        fetch_a(2)
+        fetch_a(3)
+        seats(2)
+        put_a(2)
+        put_a(3)
+        put_h(2)
+        board(2)
+        places(0)
+        places(1)
+        seats(3)
+        put_h(3)
+        board(3)
+        places(2)
+        places(3)
+
+        hid = sb("hid", [P, O * PACK], BF16)
+        nc.scalar.activation(
+            out=hid[:].rearrange("p (c i t) -> p c t i", t=PACK, i=4),
+            in_=diff[:].rearrange("p t (c i) -> p c t i", i=4),
+            func=ACT.Abs,
+        )
+        hid_codes = sb("hid_codes", [P, O], U32)
+        hid_scale = sb("hid_scale", [P, O], U8)
+        nc.vector.quantize_mx(out=hid_codes[:].bitcast(E4M3), scales=hid_scale[:], in_=hid[:])
+        for h in range(N // P):
+            nc.tensor.matmul_mx(
+                out=y_ps[h][:], lhsT=wb_raw[:].bitcast(U8)[:, 2 * P * h : 2 * P * (h + 1)].bitcast(E2M1),
+                lhsT_scale=wb_plane[:].bitcast(U8)[:, P * h : P * (h + 1)],
+                rhs=hid_codes[:].bitcast(E4M3), rhs_scale=hid_scale[:], start=False, stop=True,
+            )
+        for h in range(N // P):
+            res = sb("res%d" % h, [P, O], F32)
+            copy_on(h == 0, res[:], y_ps[h][:])
+            (nc.sync if h == 0 else nc.scalar).dma_start(out[P * h : P * (h + 1), :], res[:])

@@ -91,7 +91,8 @@ def tile_list_leadshared_twow_further_plain_kernel(
         nc.sync.dma_start(wb_raw[:], wb_words[0].bitcast(I32))
         load_plane(nc.sync, wb_plane, wb_scales)
 
-        pw = [zero_board(nc.vector, "pw%d" % t) for t in range(PACK)]
+        pw = [zero_board(nc.vector, "pw%d" % t) for t in range(2)]
+        pv = [zero_board(nc.vector, "pv%d" % t) for t in range(PACK)]
 
         for q in range(PACK):
             nc.vector.tensor_copy(w_plane[QUAD * q : QUAD * q + PACK, :], w_stage[:, q, :])
@@ -101,11 +102,10 @@ def tile_list_leadshared_twow_further_plain_kernel(
         w_scale = [sb("w_scale%d" % t, [P, P], U8) for t in range(PACK)]
         for t in range(PACK):
             nc.scalar.copy(w_codes[t][:].bitcast(U16), w_raw[:].bitcast(U16)[:, t:R:PACK])
-        nc.vector.tensor_copy(w_scale[0][:], w_plane[:].bitcast(U8)[:, 0:R:PACK])
         xg_words = sb("xg_words", [P, J], U32)
         nc.vector.tensor_copy(xg_words[:], x_words[:].bitcast(U32).indirect(l_slot[:]))
-        for t in range(1, PACK):
-            nc.vector.tensor_copy(w_scale[t][:], w_plane[:].bitcast(U8)[:, t:R:PACK])
+        for t in range(PACK):
+            nc.gpsimd.tensor_copy(w_scale[t][:], w_plane[:].bitcast(U8)[:, t:R:PACK])
         w2_codes = sb("w2_codes", [P, R], U32)
         nc.scalar.copy(
             w2_codes[:].rearrange("p (t c i) -> p c t i", t=PACK, i=4),
@@ -127,8 +127,7 @@ def tile_list_leadshared_twow_further_plain_kernel(
         a_sb = {}
         b_sb = [sb("b_sb%d" % t, [P, J], F32) for t in range(PACK)]
         h_sb = {}
-        pv = [zero_board(nc.gpsimd, "pv%d" % t, "w_codes%d" % t) for t in range(PACK)]
-        pg = [sb("pg%d" % t, [P, C], F32) for t in range(PACK)]
+        pg = {}
         g5 = [sb("g5_%d" % t, [P, O], F32) for t in range(PACK)]
         diff = sb("diff", [P, PACK, O], F32)
 
@@ -145,26 +144,27 @@ def tile_list_leadshared_twow_further_plain_kernel(
                 out=acc[:], lhsT=w2_codes[:, cols].bitcast(E4M3), lhsT_scale=w2_scale[t][:],
                 rhs=xg_words[:].bitcast(E5M2), rhs_scale=xg_scale[:], start=True, stop=True,
             )
-            nc.vector.tensor_copy(b_sb[t][:], acc[:])
+            copy_on(t >= 2, b_sb[t][:], acc[:])
 
         def fetch_a(t):
-            a_sb[t] = sb("a_sb%d" % t, [P, J], F32, "h_sb%d" % (t - 2) if t >= 2 else None)
-            copy_on(t % 2 == 0, a_sb[t][:], a_ps[t][:])
+            a_sb[t] = sb("a_sb%d" % t, [P, J], F32)
+            copy_on(t % 2 == 1, a_sb[t][:], a_ps[t][:])
 
         def put_a(t):
-            copy_on(t % 2 == 0, pw[t][:].indirect(l_put_a[:]), a_sb[t][:])
+            copy_on(t % 2 == 1, pw[t][:].indirect(l_put_a[:]), a_sb[t][:])
 
         def seats(t):
-            h_sb[t] = sb("h_sb%d" % t, [P, I], F32, "b_sb1" if t == PACK - 1 else None)
+            h_sb[t] = sb("h_sb%d" % t, [P, I], F32)
             nc.scalar.activation(
                 out=h_sb[t][:], in_=b_sb[t][:].indirect(l_seat[:]), func=ACT.Copy, scale=a_sb[t][:, 0:1]
             )
 
         def put_h(t):
-            copy_on(t % 2 == 0, pv[t][:].indirect(l_put_h[:]), h_sb[t][:])
+            copy_on(t in (1, 2), pv[t][:].indirect(l_put_h[:]), h_sb[t][:])
 
         def board(t):
-            eng = nc.vector if t == PACK - 1 else nc.gpsimd
+            eng = nc.vector if t >= 2 else nc.gpsimd
+            pg[t] = sb("pg%d" % t, [P, C], F32, {2: "pw0", 3: "pv0"}.get(t))
             eng.tensor_tensor(pg[t][:], pw[t][:], pv[t][:], ALU.add)
 
         def places(t):
@@ -177,8 +177,12 @@ def tile_list_leadshared_twow_further_plain_kernel(
         fetch_a(1)
         put_a(0)
         put_a(1)
+        fetch_a(2)
+        fetch_a(3)
         for t in range(PACK):
             second_product(t)
+        for t in (2, 3):
+            pw.append(zero_board(nc.gpsimd, "pw%d" % t, {2: "w2_scale3", 3: "w2_codes"}[t]))
 
         xs_scale = sb("xs_scale", [P, O], U8, "w_scale0")
         nc.vector.tensor_copy(xs_scale[:], x_plane[:].bitcast(U8).indirect(l_short[:]))
@@ -200,20 +204,16 @@ def tile_list_leadshared_twow_further_plain_kernel(
         put_h(1)
         board(0)
         board(1)
-        fetch_a(2)
-        fetch_a(3)
         seats(2)
+        seats(3)
+        put_h(2)
         put_a(2)
         put_a(3)
-        put_h(2)
-        board(2)
-        places(0)
-        places(1)
-        seats(3)
         put_h(3)
+        board(2)
         board(3)
-        places(2)
-        places(3)
+        for t in range(PACK):
+            places(t)
 
         hid = sb("hid", [P, O * PACK], BF16)
         nc.scalar.activation(

from contextlib import ExitStack

import concourse.mybir as mybir

K, T, J, R, C, I, O, N = 512, 1024, 256, 512, 512, 128, 128, 256
FLOPS = 2 * K * R * J * 2 + 2 * R * N * O + 2 * K * N * O

F32 = mybir.dt.float32
BF16 = mybir.dt.bfloat16
I32 = mybir.dt.int32
U32 = mybir.dt.uint32
U16 = mybir.dt.uint16
U8 = mybir.dt.uint8
E4M3 = mybir.dt.float8_e4m3fn_x4
E5M2 = mybir.dt.float8_e5m2_x4
E2M1 = mybir.dt.float4_e2m1fn_x4
ACT = mybir.ActivationFunctionType
ALU = mybir.AluOpType

P = 128
PACK = 4
QUAD = 32


def tile_list_leadshared_twow_further_plain_kernel(
    tc, xt_words, xt_scales, w_words, w_scales, w2_words, w2_scales, wb_words, wb_scales,
    ws_words, ws_scales, offs, offs2, offs3, offs4, offs5, offs6, offs7, out,
):
    nc = tc.nc
    with ExitStack() as ctx:
        keep = ctx.enter_context(tc.tile_pool(name="keep", bufs=1))
        psum = ctx.enter_context(tc.psum_pool(name="psum", bufs=1))

        def sb(name, shape, dtype, tag=None):
            return keep.tile(shape, dtype, name=name, tag=tag or name, align_bytes=64)

        def load_list(name, src):
            lst = sb(name, list(src.shape), U16)
            nc.sync.dma_start(lst[:], src)
            return lst

        def zero_plane(name, width):
            plane = sb(name, [P, width // 4], I32)
            nc.vector.memset(plane[:], 0)
            return plane

        def load_plane(queue, plane, scales):
            rows = scales[0].bitcast(I32).rearrange("(q r) n -> r q n", r=PACK)
            for r in range(PACK):
                queue.dma_start(plane[r:P:QUAD, :], rows[r])

        def load_full_plane(queue, name, scales):
            rows = scales[0].bitcast(I32)
            plane = sb(name, [P, rows.shape[1]], I32)
            for q in range(PACK):
                queue.dma_start(
                    plane[QUAD * q : QUAD * (q + 1), :],
                    rows[PACK * q : PACK * (q + 1), :].partition_broadcast(QUAD // PACK),
                )
            return plane

        def zero_board(eng, name, tag=None):
            board = sb(name, [P, C], F32, tag)
            eng.memset(board[:], 0.0)
            return board

        w_plane = zero_plane("w_plane", R)
        l_slot = load_list("l_slot", offs)
        w_stage = sb("w_stage", [PACK, PACK, R // 4], I32)
        nc.scalar.dma_start(w_stage[:], w_scales[0].bitcast(I32).rearrange("(q r) n -> r q n", r=PACK))
        x_plane = load_full_plane(nc.sync, "x_plane", xt_scales)
        x_words = sb("x_words", [P, T], I32)
        nc.scalar.dma_start(x_words[:], xt_words[0].rearrange("p n t -> p (n t)").bitcast(I32))
        w_raw = sb("w_raw", [P, R // 2], I32)
        nc.scalar.dma_start(w_raw[:], w_words[0].bitcast(I32))
        l_put_a = load_list("l_put_a", offs2)
        l_short = load_list("l_short", offs7)
        w2_raw = sb("w2_raw", [P, R], I32)
        nc.sync.dma_start(w2_raw[:], w2_words[0].rearrange("p n t -> p (n t)").bitcast(I32))
        w2_plane = load_full_plane(nc.sync, "w2_plane", w2_scales)
        l_seat = load_list("l_seat", offs3)
        l_put_h = load_list("l_put_h", offs4)
        ws_plane = sb("ws_plane", [P, N // 4], I32)
        wb_plane = sb("wb_plane", [P, N // 4], I32)
        ws_raw = sb("ws_raw", [P, N // 2], I32)
        nc.sync.dma_start(ws_raw[:], ws_words[0].bitcast(I32))
        load_plane(nc.sync, ws_plane, ws_scales)
        l_scaled = load_list("l_scaled", offs5)
        l_plain = load_list("l_plain", offs6)
        wb_raw = sb("wb_raw", [P, N // 2], I32)
        nc.sync.dma_start(wb_raw[:], wb_words[0].bitcast(I32))
        load_plane(nc.sync, wb_plane, wb_scales)

        pw = [zero_board(nc.vector, "pw%d" % t) for t in range(2)]
        pv = [zero_board(nc.vector, "pv%d" % t) for t in range(PACK)]

        for q in range(PACK):
            nc.vector.tensor_copy(w_plane[QUAD * q : QUAD * q + PACK, :], w_stage[:, q, :])
        xg_scale = sb("xg_scale", [P, J], U8)
        nc.vector.tensor_copy(xg_scale[:], x_plane[:].bitcast(U8).indirect(l_slot[:]))
        w_codes = [sb("w_codes%d" % t, [P, 2 * P], U8) for t in range(PACK)]
        w_scale = [sb("w_scale%d" % t, [P, P], U8) for t in range(PACK)]
        for t in range(PACK):
            nc.scalar.copy(w_codes[t][:].bitcast(U16), w_raw[:].bitcast(U16)[:, t:R:PACK])
        xg_words = sb("xg_words", [P, J], U32)
        nc.vector.tensor_copy(xg_words[:], x_words[:].bitcast(U32).indirect(l_slot[:]))
        for t in range(PACK):
            nc.gpsimd.tensor_copy(w_scale[t][:], w_plane[:].bitcast(U8)[:, t:R:PACK])
        w2_codes = sb("w2_codes", [P, R], U32)
        nc.scalar.copy(
            w2_codes[:].rearrange("p (t c i) -> p c t i", t=PACK, i=4),
            w2_raw[:].bitcast(U32).rearrange("p (c i t) -> p c t i", t=PACK, i=4),
        )
        w2_scale = [sb("w2_scale%d" % t, [P, P], U8) for t in range(PACK)]
        for t in range(PACK):
            nc.gpsimd.tensor_copy(w2_scale[t][:], w2_plane[:].bitcast(U8)[:, t:R:PACK])

        a_ps = []
        for t in range(PACK):
            acc = psum.tile([P, J], F32, name="a_ps%d" % t, tag="bank%d" % t)
            nc.tensor.matmul_mx(
                out=acc[:], lhsT=w_codes[t][:].bitcast(E2M1), lhsT_scale=w_scale[t][:],
                rhs=xg_words[:].bitcast(E5M2), rhs_scale=xg_scale[:], start=True, stop=True,
            )
            a_ps.append(acc)

        a_sb = {}
        b_sb = [sb("b_sb%d" % t, [P, J], F32) for t in range(PACK)]
        h_sb = {}
        pg = {}
        g5 = [sb("g5_%d" % t, [P, O], F32) for t in range(PACK)]
        diff = sb("diff", [P, PACK, O], F32)

        def copy_on(on_vector, dst, src):
            if on_vector:
                nc.vector.tensor_copy(dst, src)
            else:
                nc.scalar.activation(out=dst, in_=src, func=ACT.Copy)

        def second_product(t):
            acc = psum.tile([P, J], F32, name="b_ps%d" % t, tag="bank%d" % ((t + 4) % 6))
            cols = slice(P * t, P * (t + 1))
            nc.tensor.matmul_mx(
                out=acc[:], lhsT=w2_codes[:, cols].bitcast(E4M3), lhsT_scale=w2_scale[t][:],
                rhs=xg_words[:].bitcast(E5M2), rhs_scale=xg_scale[:], start=True, stop=True,
            )
            copy_on(t >= 2, b_sb[t][:], acc[:])

        def fetch_a(t):
            a_sb[t] = sb("a_sb%d" % t, [P, J], F32)
            copy_on(t % 2 == 1, a_sb[t][:], a_ps[t][:])

        def put_a(t):
            copy_on(t % 2 == 1, pw[t][:].indirect(l_put_a[:]), a_sb[t][:])

        def seats(t):
            h_sb[t] = sb("h_sb%d" % t, [P, I], F32)
            nc.scalar.activation(
                out=h_sb[t][:], in_=b_sb[t][:].indirect(l_seat[:]), func=ACT.Copy, scale=a_sb[t][:, 0:1]
            )

        def put_h(t):
            copy_on(t in (1, 2), pv[t][:].indirect(l_put_h[:]), h_sb[t][:])

        def board(t):
            eng = nc.vector if t >= 2 else nc.gpsimd
            pg[t] = sb("pg%d" % t, [P, C], F32, {2: "pw0", 3: "pv0"}.get(t))
            eng.tensor_tensor(pg[t][:], pw[t][:], pv[t][:], ALU.add)

        def places(t):
            nc.scalar.activation(
                out=g5[t][:], in_=pg[t][:].indirect(l_scaled[:]), func=ACT.Copy, scale=b_sb[t][:, 0:1]
            )
            nc.vector.tensor_tensor(diff[:, t, :], pg[t][:].indirect(l_plain[:]), g5[t][:], ALU.subtract)

        fetch_a(0)
        fetch_a(1)
        put_a(0)
        put_a(1)
        fetch_a(2)
        fetch_a(3)
        for t in range(PACK):
            second_product(t)
        for t in (2, 3):
            pw.append(zero_board(nc.gpsimd, "pw%d" % t, {2: "w2_scale3", 3: "w2_codes"}[t]))

        xs_scale = sb("xs_scale", [P, O], U8, "w_scale0")
        nc.vector.tensor_copy(xs_scale[:], x_plane[:].bitcast(U8).indirect(l_short[:]))
        xs_words = sb("xs_words", [P, O], U32)
        nc.vector.tensor_copy(xs_words[:], x_words[:].bitcast(U32).indirect(l_short[:]))
        y_ps = []
        for h in range(N // P):
            acc = psum.tile([P, O], F32, name="y_ps%d" % h, tag="out_bank%d" % h)
            nc.tensor.matmul_mx(
                out=acc[:], lhsT=ws_raw[:].bitcast(U8)[:, 2 * P * h : 2 * P * (h + 1)].bitcast(E2M1),
                lhsT_scale=ws_plane[:].bitcast(U8)[:, P * h : P * (h + 1)],
                rhs=xs_words[:].bitcast(E5M2), rhs_scale=xs_scale[:], start=True, stop=False,
            )
            y_ps.append(acc)

        seats(0)
        seats(1)
        put_h(0)
        put_h(1)
        board(0)
        board(1)
        seats(2)
        seats(3)
        put_h(2)
        put_a(2)
        put_a(3)
        put_h(3)
        board(2)
        board(3)
        for t in range(PACK):
            places(t)

        hid = sb("hid", [P, O * PACK], BF16)
        nc.scalar.activation(
            out=hid[:].rearrange("p (c i t) -> p c t i", t=PACK, i=4),
            in_=diff[:].rearrange("p t (c i) -> p c t i", i=4),
            func=ACT.Abs,
        )
        hid_codes = sb("hid_codes", [P, O], U32)
        hid_scale = sb("hid_scale", [P, O], U8)
        nc.vector.quantize_mx(out=hid_codes[:].bitcast(E4M3), scales=hid_scale[:], in_=hid[:])
        for h in range(N // P):
            nc.tensor.matmul_mx(
                out=y_ps[h][:], lhsT=wb_raw[:].bitcast(U8)[:, 2 * P * h : 2 * P * (h + 1)].bitcast(E2M1),
                lhsT_scale=wb_plane[:].bitcast(U8)[:, P * h : P * (h + 1)],
                rhs=hid_codes[:].bitcast(E4M3), rhs_scale=hid_scale[:], start=False, stop=True,
            )
        for h in range(N // P):
            res = sb("res%d" % h, [P, O], F32)
            copy_on(h == 0, res[:], y_ps[h][:])
            (nc.sync if h == 0 else nc.scalar).dma_start(out[P * h : P * (h + 1), :], res[:])
